import numpy as np
import ml_dtypes


def mxq(x, axis, fmt="e4m3"):
    dtype, down = {"e4m3": (ml_dtypes.float8_e4m3fn, 7), "e5m2": (ml_dtypes.float8_e5m2, 14)}[fmt]
    v = np.moveaxis(np.asarray(x, np.float32).astype(ml_dtypes.bfloat16).astype(np.float64), axis, -1)
    blocks = v.reshape(v.shape[:-1] + (-1, 32))
    amax = np.abs(blocks).max(-1, keepdims=True)
    byte = np.maximum(np.where(amax > 0, np.frexp(amax)[1] - 1 + 127, 0) - down, 1)
    scale = np.exp2(byte - 127.0)
    codes = (blocks / scale).astype(np.float32).astype(dtype).astype(np.float64)
    return np.moveaxis((codes * scale).reshape(v.shape), -1, axis)


WIDE = False


def mx_kscale(k):
    if not WIDE:
        return np.ones(k)
    levels = np.array([10, -10, 5, -5, 0])
    if k % 512:
        return np.exp2(np.random.permutation(np.resize(levels, k // 32))).repeat(32)
    a = np.empty((k // 512, 16))
    for p in range(k // 512):
        a[p, :8] = np.random.permutation(np.resize(levels, 8))
        for g in range(8):
            far = levels[np.abs(levels - a[p, g]) >= 10]
            a[p, g + 8] = far[np.random.randint(len(far))]
    return np.exp2(a.ravel()).repeat(32)


def f64(x):
    return np.asarray(x).astype(np.float64)


def striped8(idx):
    return np.asarray(idx).reshape(8, -1, 16).transpose(0, 2, 1).reshape(128, -1).astype(np.uint16)


def unstriped8(offs):
    return offs.reshape(8, 16, -1).transpose(0, 2, 1).reshape(8, -1).astype(np.int64)


def pick8(x, idx, run):
    r = np.arange(len(x))
    return x[r[:, None], idx[r % (8 * run) // run]]


E2M1 = np.array([0.0, 0.5, 1.0, 1.5, 2.0, 3.0, 4.0, 6.0, -0.0, -0.5, -1.0, -1.5, -2.0, -3.0, -4.0, -6.0])


def pack_weight(w, fmt):
    k, n = w.shape
    w = f64(np.asarray(w, np.float32).astype(ml_dtypes.bfloat16)).reshape(k // 32, 32, n)
    amax = np.abs(w).max(1)
    if fmt == "e4m3":
        byte = np.frexp(amax)[1] - 1 + 127 - 7
    else:
        mant, ex = np.frexp(amax / 6.0)
        byte = np.where(mant > 0.5, ex, ex - 1) + 127
    byte = np.clip(np.where(amax > 0, byte, 1), 1, 254)
    scaled = (w * np.exp2(127.0 - byte)[:, None, :]).reshape(k, n).astype(np.float32)
    by_word = np.ascontiguousarray(scaled.reshape(k // 512, 128, 4, n).transpose(0, 1, 3, 2))
    if fmt == "e4m3":
        words = by_word.astype(ml_dtypes.float8_e4m3fn).view(np.uint8)
    else:
        c = by_word.astype(ml_dtypes.float4_e2m1fn).view(np.uint8) & 0xF
        words = (c[..., 0::2] | (c[..., 1::2] << 4)).reshape(k // 512, 128, 2 * n)
    return np.ascontiguousarray(words), np.ascontiguousarray(byte.astype(np.uint8).reshape(k // 512, 16, n))


def unpack_weight(words, scales, fmt):
    g, _, n = scales.shape
    words = np.ascontiguousarray(words).reshape(g, 128, n, -1)
    if fmt == "e4m3":
        vals = words.view(ml_dtypes.float8_e4m3fn).astype(np.float64)
    else:
        nib = np.empty((g, 128, n, 4), np.uint8)
        nib[..., 0::2] = words & 0xF
        nib[..., 1::2] = words >> 4
        vals = E2M1[nib]
    vals = vals * np.repeat(np.exp2(scales.astype(np.float64) - 127.0), 8, axis=1)[..., None]
    return vals.transpose(0, 1, 3, 2).reshape(g * 512, n)


D, T, U, I, J, Q, E = 512, 1024, 1024, 512, 256, 512, 256


def setup_inputs():
    n = np.random.standard_normal
    idx = np.stack([np.random.permutation(T)[:I] for _ in range(8)])
    idx2 = np.stack([np.random.permutation(U)[:I] for _ in range(8)])
    idx3 = np.stack([np.random.permutation(U)[:J] for _ in range(8)])
    idx4 = np.stack([np.random.permutation(U)[:I] for _ in range(8)])
    fd = mx_kscale(D)
    fq = mx_kscale(Q)
    keysp = pack_weight(n((D, T)) / fd[:, None], "e2m1")
    notesp = pack_weight(n((D, U)) / fd[:, None], "e4m3")
    mixp = pack_weight(n((Q, E)) * 1.0 / np.sqrt(Q) / fq[:, None], "e4m3")
    return {
        "query": (n((D, Q)) * 1.0 / np.sqrt(D) * fd[:, None]).astype(np.float32),
        "query2": (n((D, Q)) * 1.0 / np.sqrt(D) * fd[:, None]).astype(np.float32),
        "keys_words": keysp[0],
        "keys_scales": keysp[1],
        "notes_words": notesp[0],
        "notes_scales": notesp[1],
        "rowf": (np.random.uniform(0.5, 2.0, (Q, 1)) * fq[:, None]).astype(np.float32),
        "mix_words": mixp[0],
        "mix_scales": mixp[1],
        "offs": striped8(idx),
        "offs2": striped8(idx2),
        "offs3": striped8(idx3),
        "offs4": striped8(idx4),
    }


def reference(query, query2, keys_words, keys_scales, notes_words, notes_scales, rowf, mix_words, mix_scales, offs, offs2, offs3, offs4):
    idx = unstriped8(offs)
    idx2 = unstriped8(offs2)
    idx3 = unstriped8(offs3)
    idx4 = unstriped8(offs4)
    keysu = unpack_weight(keys_words, keys_scales, "e2m1")
    notesu = unpack_weight(notes_words, notes_scales, "e4m3")
    mixu = unpack_weight(mix_words, mix_scales, "e4m3")
    queryq = mxq(f64(query), 0, "e4m3")
    a = queryq.T @ keysu
    query2q = mxq(f64(query2), 0, "e4m3")
    b = query2q.T @ notesu
    w = pick8(a, idx, 64) + pick8(b, idx2, 64)
    m2 = w.reshape(Q, J, I // J).max(axis=2)
    f1 = np.zeros((Q, U))
    f1[np.arange(Q)[:, None], idx3[np.arange(Q) % 512 // 64]] = m2
    cc = b + f1
    g = pick8(cc, idx4, 64) - w
    gw = g * f64(rowf)
    gwq = mxq(gw, 0, "e4m3")
    y = mixu.T @ gwq
    return y

@@ -1,0 +1,240 @@
+from contextlib import ExitStack
+
+import concourse.mybir as mybir
+
+D, T, U, I, J, Q, E = 512, 1024, 1024, 512, 256, 512, 256
+FLOPS = 2 * D * Q * T + 2 * D * Q * U + 2 * Q * E * I
+
+F32 = mybir.dt.float32
+BF16 = mybir.dt.bfloat16
+I32 = mybir.dt.int32
+U32 = mybir.dt.uint32
+U16 = mybir.dt.uint16
+U8 = mybir.dt.uint8
+FP8X4 = mybir.dt.float8_e4m3fn_x4
+FP4X4 = mybir.dt.float4_e2m1fn_x4
+ALU = mybir.AluOpType
+COPY = mybir.ActivationFunctionType.Copy
+
+P = 128
+PACK = 4
+BANK = 512
+HALVES = 2
+
+
+def tile_attend_pairwinners_twoq_mixed_kernel(
+    tc, query, query2, keys_words, keys_scales, notes_words, notes_scales, rowf,
+    mix_words, mix_scales, offs, offs2, offs3, offs4, out,
+):
+    nc = tc.nc
+    with ExitStack() as ctx:
+        keep = ctx.enter_context(tc.tile_pool(name="keep", bufs=1))
+        psum = ctx.enter_context(tc.psum_pool(name="psum", bufs=8))
+
+        def zeroed_plane(engine, name, width):
+            plane = keep.tile([P, width], U8, name=name, align_bytes=64)
+            engine.memset(plane[:].bitcast(I32), 0)
+            return plane
+
+        def load_scales(queue, plane, scales):
+            for quad in range(4):
+                queue.dma_start(
+                    out=plane[32 * quad : 32 * quad + 4, :].bitcast(I32),
+                    in_=scales[0, 4 * quad : 4 * quad + 4, :].bitcast(I32),
+                )
+
+        def load_query(name, src):
+            rows = src.rearrange("(p j) q -> p j q", j=PACK)
+            halves = []
+            for h in range(HALVES):
+                raw = keep.tile([P, PACK, Q // HALVES], F32, name=f"{name}_raw{h}")
+                nc.sync.dma_start(out=raw[:], in_=rows[:, :, h * Q // HALVES : (h + 1) * Q // HALVES])
+                halves.append(raw)
+            return halves
+
+        def load_list(name, src, n):
+            lst = keep.tile([P, n // 16], U16, name=name)
+            nc.sync.dma_start(lst[:], src)
+            return lst
+
+        keys_plane = zeroed_plane(nc.vector, "keys_plane", T)
+        notes_plane = zeroed_plane(nc.vector, "notes_plane", U)
+        mix_plane = zeroed_plane(nc.gpsimd, "mix_plane", E)
+        placed = []
+        for n in range(2):
+            f1 = keep.tile([P, U], F32, name=f"placed{n}")
+            nc.vector.memset(f1[:], 0.0)
+            placed.append(f1)
+
+        load_scales(nc.scalar, keys_plane, keys_scales)
+        load_scales(nc.gpsimd, mix_plane, mix_scales)
+        q1_raw = load_query("q1", query)
+        keys = keep.tile([P, 2 * T], U8, name="keys", align_bytes=64)
+        nc.sync.dma_start(out=keys[:].bitcast(I32), in_=keys_words[0].bitcast(I32))
+        list_a = load_list("list_a", offs, I)
+        q2_raw = load_query("q2", query2)
+        load_scales(nc.sync, notes_plane, notes_scales)
+        list_b = load_list("list_b", offs2, I)
+        notes = keep.tile([P, U], U32, name="notes", align_bytes=64)
+        nc.sync.dma_start(
+            out=notes[:].bitcast(I32), in_=notes_words[0].rearrange("p n t -> p (n t)").bitcast(I32)
+        )
+        list_f = load_list("list_f", offs3, J)
+        list_c = load_list("list_c", offs4, I)
+        factor = keep.tile([P, PACK], F32, name="factor")
+        nc.sync.dma_start(out=factor[:], in_=rowf.rearrange("(p t) o -> p (t o)", t=PACK))
+        mix = keep.tile([P, E], U32, name="mix", align_bytes=64)
+        nc.sync.dma_start(
+            out=mix[:].bitcast(I32), in_=mix_words[0].rearrange("p n t -> p (n t)").bitcast(I32)
+        )
+
+        def quantise_query(name, halves):
+            grouped = keep.tile([P, PACK, P, PACK], BF16, name=f"{name}_grouped", align_bytes=64)
+            per = P // HALVES
+            for h, raw in enumerate(halves):
+                nc.vector.tensor_copy(
+                    out=grouped[:, :, h * per : (h + 1) * per, :].rearrange("p t m j -> p m j t"),
+                    in_=raw[:].rearrange("p j (m t) -> p m j t", t=PACK),
+                )
+            codes = keep.tile([P, Q], U32, name=f"{name}_codes", align_bytes=64)
+            plane = keep.tile([P, Q], U8, name=f"{name}_plane", align_bytes=64)
+            flat = grouped[:].rearrange("p t m j -> p (t m j)")
+            for t in range(PACK):
+                cols = slice(t * P, (t + 1) * P)
+                nc.vector.quantize_mx(
+                    out=codes[:, cols].bitcast(FP8X4),
+                    scales=plane[:, cols],
+                    in_=flat[:, PACK * cols.start : PACK * cols.stop],
+                )
+            return codes, plane
+
+        def scores(name, t, codes, plane, moving, moving_plane, shared):
+            whole = keep.tile([P, T], F32, name=f"{name}{t}")
+            rows = slice(t * P, (t + 1) * P)
+            for c in range(T // BANK):
+                cols = slice(c * BANK, (c + 1) * BANK)
+                acc = psum.tile([P, BANK], F32, name="acc")
+                nc.tensor.matmul_mx(
+                    out=acc[:],
+                    lhsT=codes[:, rows].bitcast(FP8X4),
+                    lhsT_scale=plane[:, rows],
+                    rhs=moving(cols),
+                    rhs_scale=moving_plane[:, cols],
+                    start=True,
+                    stop=True,
+                )
+                if shared and c == 1:
+                    nc.vector.tensor_copy(whole[:, cols], acc[:])
+                else:
+                    nc.scalar.activation(whole[:, cols], acc[:], COPY)
+            return whole
+
+        def token_bids(t, shared=False):
+            a = scores("a", t, q1_codes, q1_plane,
+                       lambda cols: keys[:, 2 * cols.start : 2 * cols.stop].bitcast(FP4X4), keys_plane, shared)
+            ga = keep.tile([P, I], F32, name=f"ga{t}")
+            nc.scalar.activation(ga[:], a[:].indirect(list_a[:]), COPY)
+            return ga
+
+        def note_scores(t, shared=False):
+            return scores("b", t, q2_codes, q2_plane, lambda cols: notes[:, cols].bitcast(FP8X4), notes_plane, shared)
+
+        def note_bids(t, b):
+            gb = keep.tile([P, I], F32, name=f"gb{t}")
+            nc.scalar.activation(gb[:], b[:].indirect(list_b[:]), COPY)
+            return gb[:]
+
+        def bids(t, looked_up, ga):
+            w = keep.tile([P, I], F32, name=f"w{t}")
+            nc.vector.tensor_tensor(w[:], looked_up, ga[:], ALU.add)
+            return w
+
+        def winners(t, w):
+            m2 = keep.tile([P, J], F32, name=f"m2_{t}")
+            pairs = w[:].rearrange("p (j two) -> p j two", two=2)
+            nc.vector.tensor_tensor(m2[:], pairs[:, :, 0], pairs[:, :, 1], ALU.max)
+            return m2
+
+        def place(t, m2):
+            nc.vector.tensor_copy(placed[t % 2][:].indirect(list_f[:]), m2[:])
+
+        def raise_notes(t, b):
+            cc = keep.tile([P, U], F32, name=f"cc{t}")
+            nc.vector.tensor_tensor(cc[:], b[:], placed[t % 2][:], ALU.add)
+            return cc
+
+        planes = keep.tile([P, PACK, I], BF16, name="planes")
+
+        def standing(cc, cols):
+            return cc[:].indirect(list_c[:, cols.start // 16 : cols.stop // 16])
+
+        def fetch(name, cc, cols):
+            gc = keep.tile([P, cols.stop - cols.start], F32, name=name)
+            nc.scalar.activation(gc[:], standing(cc, cols), COPY)
+            return gc[:]
+
+        def results(name, t, looked_up, w, cols):
+            g = keep.tile([P, cols.stop - cols.start], F32, name=name)
+            nc.vector.tensor_tensor(g[:], looked_up, w[:, cols], ALU.subtract)
+            nc.scalar.activation(planes[:, t, cols], g[:], COPY, scale=factor[:, t : t + 1])
+
+        every = slice(0, I)
+        q1_codes, q1_plane = quantise_query("q1", q1_raw)
+        ga = {0: token_bids(0, True), 1: token_bids(1, True)}
+        q2_codes, q2_plane = quantise_query("q2", q2_raw)
+        b = {0: note_scores(0, True)}
+        w = {0: bids(0, b[0][:].indirect(list_b[:]), ga[0])}
+        b[1] = note_scores(1)
+        gb = {1: note_bids(1, b[1])}
+        cc = {}
+        gc = {}
+        last = PACK - 1
+        for t in range(PACK):
+            m2 = winners(t, w[t])
+            if t + 2 < PACK:
+                ga[t + 2] = token_bids(t + 2)
+                b[t + 2] = note_scores(t + 2)
+                gb[t + 2] = note_bids(t + 2, b[t + 2])
+            place(t, m2)
+            if t > 0:
+                gc[t - 1] = fetch(f"gc{t - 1}", cc[t - 1], every)
+            if t < last:
+                w[t + 1] = bids(t + 1, gb[t + 1], ga[t + 1])
+            if t > 1:
+                results(f"g{t - 2}", t - 2, gc[t - 2], w[t - 2], every)
+            cc[t] = raise_notes(t, b[t])
+        first, second = slice(0, I // 2), slice(I // 2, I)
+        fetched = fetch("gc_second", cc[last], second)
+        results(f"g{last - 1}", last - 1, gc[last - 1], w[last - 1], every)
+        results("g_first", last, standing(cc[last], first), w[last], first)
+        results("g_second", last, fetched, w[last], second)
+
+        n = I // HALVES
+        out_rows = out.rearrange("(c p) i -> p c i", p=P)
+        for h in range(HALVES):
+            cols = slice(h * n, (h + 1) * n)
+            grouped = keep.tile([P, n, PACK], BF16, name=f"gw_grouped{h}", align_bytes=64)
+            nc.vector.tensor_copy(
+                out=grouped[:].rearrange("p (c i) t -> p c t i", i=4),
+                in_=planes[:, :, cols].rearrange("p t (c i) -> p c t i", i=4),
+            )
+            codes = keep.tile([P, n], U32, name=f"gw_codes{h}", align_bytes=64)
+            plane = keep.tile([P, n], U8, name=f"gw_plane{h}", align_bytes=64)
+            nc.vector.quantize_mx(
+                out=codes[:].bitcast(FP8X4), scales=plane[:], in_=grouped[:].rearrange("p i t -> p (i t)")
+            )
+            acc = psum.tile([P, E // P, n], F32, name="acc")
+            for c in range(E // P):
+                chans = slice(c * P, (c + 1) * P)
+                nc.tensor.matmul_mx(
+                    out=acc[:, c, :],
+                    lhsT=mix[:, chans].bitcast(FP8X4),
+                    lhsT_scale=mix_plane[:, chans],
+                    rhs=codes[:].bitcast(FP8X4),
+                    rhs_scale=plane[:],
+                    start=True,
+                    stop=True,
+                )
+            result = keep.tile([P, E // P, n], F32, name=f"result{h}")
+            nc.scalar.activation(result[:], acc[:], COPY)
+            nc.sync.dma_start(out=out_rows[:, :, cols], in_=result[:])

@@ -29,7 +29,7 @@ def tile_attend_pairwinners_twoq_mixed_kernel(
     nc = tc.nc
     with ExitStack() as ctx:
         keep = ctx.enter_context(tc.tile_pool(name="keep", bufs=1))
-        psum = ctx.enter_context(tc.psum_pool(name="psum", bufs=8))
+        psum = ctx.enter_context(tc.psum_pool(name="psum", bufs=1))
 
         def zeroed_plane(engine, name, width):
             plane = keep.tile([P, width], U8, name=name, align_bytes=64)
@@ -47,8 +47,8 @@ def tile_attend_pairwinners_twoq_mixed_kernel(
             rows = src.rearrange("(p j) q -> p j q", j=PACK)
             halves = []
             for h in range(HALVES):
-                raw = keep.tile([P, PACK, Q // HALVES], F32, name=f"{name}_raw{h}")
-                nc.sync.dma_start(out=raw[:], in_=rows[:, :, h * Q // HALVES : (h + 1) * Q // HALVES])
+                raw = keep.tile([P, 2, Q], F32, name=f"{name}_raw{h}")
+                nc.sync.dma_start(out=raw[:], in_=rows[:, 2 * h : 2 * h + 2, :])
                 halves.append(raw)
             return halves
 
@@ -59,7 +59,7 @@ def tile_attend_pairwinners_twoq_mixed_kernel(
 
         keys_plane = zeroed_plane(nc.vector, "keys_plane", T)
         notes_plane = zeroed_plane(nc.vector, "notes_plane", U)
-        mix_plane = zeroed_plane(nc.gpsimd, "mix_plane", E)
+        mix_plane = zeroed_plane(nc.vector, "mix_plane", E)
         placed = []
         for n in range(2):
             f1 = keep.tile([P, U], F32, name=f"placed{n}")
@@ -67,7 +67,6 @@ def tile_attend_pairwinners_twoq_mixed_kernel(
             placed.append(f1)
 
         load_scales(nc.scalar, keys_plane, keys_scales)
-        load_scales(nc.gpsimd, mix_plane, mix_scales)
         q1_raw = load_query("q1", query)
         keys = keep.tile([P, 2 * T], U8, name="keys", align_bytes=64)
         nc.sync.dma_start(out=keys[:].bitcast(I32), in_=keys_words[0].bitcast(I32))
@@ -87,13 +86,13 @@ def tile_attend_pairwinners_twoq_mixed_kernel(
         nc.sync.dma_start(
             out=mix[:].bitcast(I32), in_=mix_words[0].rearrange("p n t -> p (n t)").bitcast(I32)
         )
+        load_scales(nc.sync, mix_plane, mix_scales)
 
         def quantise_query(name, halves):
             grouped = keep.tile([P, PACK, P, PACK], BF16, name=f"{name}_grouped", align_bytes=64)
-            per = P // HALVES
             for h, raw in enumerate(halves):
                 nc.vector.tensor_copy(
-                    out=grouped[:, :, h * per : (h + 1) * per, :].rearrange("p t m j -> p m j t"),
+                    out=grouped[:, :, :, 2 * h : 2 * h + 2].rearrange("p t m j -> p m j t"),
                     in_=raw[:].rearrange("p j (m t) -> p m j t", t=PACK),
                 )
             codes = keep.tile([P, Q], U32, name=f"{name}_codes", align_bytes=64)
@@ -108,12 +107,11 @@ def tile_attend_pairwinners_twoq_mixed_kernel(
                 )
             return codes, plane
 
-        def scores(name, t, codes, plane, moving, moving_plane, shared):
-            whole = keep.tile([P, T], F32, name=f"{name}{t}")
+        def scores(name, t, parts, codes, plane, moving, moving_plane, on_vector):
+            whole = keep.tile([P, T], F32, name=f"{name}{t}", tag=f"{name}{t}")
             rows = slice(t * P, (t + 1) * P)
-            for c in range(T // BANK):
-                cols = slice(c * BANK, (c + 1) * BANK)
-                acc = psum.tile([P, BANK], F32, name="acc")
+            for bank, cols in parts:
+                acc = psum.tile([P, cols.stop - cols.start], F32, name=f"acc_{name}{t}_{bank}", tag=f"bank{bank}")
                 nc.tensor.matmul_mx(
                     out=acc[:],
                     lhsT=codes[:, rows].bitcast(FP8X4),
@@ -123,21 +121,30 @@ def tile_attend_pairwinners_twoq_mixed_kernel(
                     start=True,
                     stop=True,
                 )
-                if shared and c == 1:
+                if on_vector:
                     nc.vector.tensor_copy(whole[:, cols], acc[:])
                 else:
                     nc.scalar.activation(whole[:, cols], acc[:], COPY)
             return whole
 
-        def token_bids(t, shared=False):
-            a = scores("a", t, q1_codes, q1_plane,
-                       lambda cols: keys[:, 2 * cols.start : 2 * cols.stop].bitcast(FP4X4), keys_plane, shared)
+        def pair(k):
+            return [(2 * k + c, slice(c * BANK, (c + 1) * BANK)) for c in range(2)]
+
+        def token_scores(t, on_vector=False):
+            return scores("a", t, pair(t), q1_codes, q1_plane,
+                          lambda cols: keys[:, 2 * cols.start : 2 * cols.stop].bitcast(FP4X4), keys_plane, on_vector)
+
+        def token_bids(t, a):
             ga = keep.tile([P, I], F32, name=f"ga{t}")
             nc.scalar.activation(ga[:], a[:].indirect(list_a[:]), COPY)
             return ga
 
-        def note_scores(t, shared=False):
-            return scores("b", t, q2_codes, q2_plane, lambda cols: notes[:, cols].bitcast(FP8X4), notes_plane, shared)
+        def note_scores(t, on_vector=False):
+            parts = pair((t + 2) % PACK)
+            if t == 0:
+                parts = [parts[0], (parts[1][0], slice(512, 768)), (0, slice(768, 1024))]
+            return scores("b", t, parts, q2_codes, q2_plane,
+                          lambda cols: notes[:, cols].bitcast(FP8X4), notes_plane, on_vector)
 
         def note_bids(t, b):
             gb = keep.tile([P, I], F32, name=f"gb{t}")
@@ -159,10 +166,11 @@ def tile_attend_pairwinners_twoq_mixed_kernel(
             nc.vector.tensor_copy(placed[t % 2][:].indirect(list_f[:]), m2[:])
 
         def raise_notes(t, b):
-            cc = keep.tile([P, U], F32, name=f"cc{t}")
+            cc = keep.tile([P, U], F32, name=f"cc{t}", tag=f"a{(t + 1) % PACK}")
             nc.vector.tensor_tensor(cc[:], b[:], placed[t % 2][:], ALU.add)
             return cc
 
+        n = I // HALVES
         planes = keep.tile([P, PACK, I], BF16, name="planes")
 
         def standing(cc, cols):
@@ -173,44 +181,48 @@ def tile_attend_pairwinners_twoq_mixed_kernel(
             nc.scalar.activation(gc[:], standing(cc, cols), COPY)
             return gc[:]
 
-        def results(name, t, looked_up, w, cols):
+        def results(name, looked_up, w, cols):
             g = keep.tile([P, cols.stop - cols.start], F32, name=name)
             nc.vector.tensor_tensor(g[:], looked_up, w[:, cols], ALU.subtract)
+            return g
+
+        def weigh(t, g, cols):
             nc.scalar.activation(planes[:, t, cols], g[:], COPY, scale=factor[:, t : t + 1])
 
         every = slice(0, I)
         q1_codes, q1_plane = quantise_query("q1", q1_raw)
-        ga = {0: token_bids(0, True), 1: token_bids(1, True)}
+        ga = {0: token_bids(0, token_scores(0))}
         q2_codes, q2_plane = quantise_query("q2", q2_raw)
+        ga[1] = token_bids(1, token_scores(1))
         b = {0: note_scores(0, True)}
         w = {0: bids(0, b[0][:].indirect(list_b[:]), ga[0])}
-        b[1] = note_scores(1)
-        gb = {1: note_bids(1, b[1])}
-        cc = {}
-        gc = {}
-        last = PACK - 1
-        for t in range(PACK):
-            m2 = winners(t, w[t])
-            if t + 2 < PACK:
-                ga[t + 2] = token_bids(t + 2)
-                b[t + 2] = note_scores(t + 2)
-                gb[t + 2] = note_bids(t + 2, b[t + 2])
-            place(t, m2)
-            if t > 0:
-                gc[t - 1] = fetch(f"gc{t - 1}", cc[t - 1], every)
-            if t < last:
-                w[t + 1] = bids(t + 1, gb[t + 1], ga[t + 1])
+        gb = {}
+        for t in range(1, PACK):
             if t > 1:
-                results(f"g{t - 2}", t - 2, gc[t - 2], w[t - 2], every)
-            cc[t] = raise_notes(t, b[t])
-        first, second = slice(0, I // 2), slice(I // 2, I)
-        fetched = fetch("gc_second", cc[last], second)
-        results(f"g{last - 1}", last - 1, gc[last - 1], w[last - 1], every)
-        results("g_first", last, standing(cc[last], first), w[last], first)
-        results("g_second", last, fetched, w[last], second)
+                a = token_scores(t)
+            b[t] = note_scores(t)
+            gb[t] = note_bids(t, b[t])
+            if t > 1:
+                ga[t] = token_bids(t, a)
+        last = PACK - 1
+        m2 = winners(0, w[0])
+        fetched = {}
+        for t in range(last):
+            place(t, m2)
+            w[t + 1] = bids(t + 1, gb[t + 1], ga[t + 1])
+            cc = raise_notes(t, b[t])
+            m2 = winners(t + 1, w[t + 1])
+            fetched[t] = fetch(f"gc{t}", cc, every)
+        for t in range(last):
+            if t == last - 1:
+                place(last, m2)
+            weigh(t, results(f"g{t}", fetched[t], w[t], every), every)
+        cc = raise_notes(last, b[last])
+        first, second = slice(0, n), slice(n, I)
+        fetched_second = fetch("gc_second", cc, second)
+        weigh(last, results("g_first", standing(cc, first), w[last], first), first)
+        weigh(last, results("g_second", fetched_second, w[last], second), second)
 
-        n = I // HALVES
-        out_rows = out.rearrange("(c p) i -> p c i", p=P)
         for h in range(HALVES):
             cols = slice(h * n, (h + 1) * n)
             grouped = keep.tile([P, n, PACK], BF16, name=f"gw_grouped{h}", align_bytes=64)
@@ -223,11 +235,11 @@ def tile_attend_pairwinners_twoq_mixed_kernel(
             nc.vector.quantize_mx(
                 out=codes[:].bitcast(FP8X4), scales=plane[:], in_=grouped[:].rearrange("p i t -> p (i t)")
             )
-            acc = psum.tile([P, E // P, n], F32, name="acc")
             for c in range(E // P):
                 chans = slice(c * P, (c + 1) * P)
+                acc = psum.tile([P, n], F32, name=f"acc_out{h}_{c}", tag=f"bank{2 * h + c}")
                 nc.tensor.matmul_mx(
-                    out=acc[:, c, :],
+                    out=acc[:],
                     lhsT=mix[:, chans].bitcast(FP8X4),
                     lhsT_scale=mix_plane[:, chans],
                     rhs=codes[:].bitcast(FP8X4),
@@ -235,6 +247,9 @@ def tile_attend_pairwinners_twoq_mixed_kernel(
                     start=True,
                     stop=True,
                 )
-            result = keep.tile([P, E // P, n], F32, name=f"result{h}")
-            nc.scalar.activation(result[:], acc[:], COPY)
-            nc.sync.dma_start(out=out_rows[:, :, cols], in_=result[:])
+                result = keep.tile([P, n], F32, name=f"result{h}_{c}")
+                if h == 1 and c == 1:
+                    nc.vector.tensor_copy(result[:], acc[:])
+                else:
+                    nc.scalar.activation(result[:], acc[:], COPY)
+                nc.sync.dma_start(out=out[chans, cols], in_=result[:])

@@ -109,6 +109,7 @@ def tile_attend_pairwinners_twoq_mixed_kernel(
 
         def scores(name, t, parts, codes, plane, moving, moving_plane, on_vector):
             whole = keep.tile([P, T], F32, name=f"{name}{t}", tag=f"{name}{t}")
+            banks = []
             rows = slice(t * P, (t + 1) * P)
             for bank, cols in parts:
                 acc = psum.tile([P, cols.stop - cols.start], F32, name=f"acc_{name}{t}_{bank}", tag=f"bank{bank}")
@@ -125,14 +126,15 @@ def tile_attend_pairwinners_twoq_mixed_kernel(
                     nc.vector.tensor_copy(whole[:, cols], acc[:])
                 else:
                     nc.scalar.activation(whole[:, cols], acc[:], COPY)
-            return whole
+                banks.append((cols, acc))
+            return whole, banks
 
         def pair(k):
             return [(2 * k + c, slice(c * BANK, (c + 1) * BANK)) for c in range(2)]
 
         def token_scores(t, on_vector=False):
-            return scores("a", t, pair(t), q1_codes, q1_plane,
-                          lambda cols: keys[:, 2 * cols.start : 2 * cols.stop].bitcast(FP4X4), keys_plane, on_vector)
+            return scores("a", t, pair(min(t, 2)), q1_codes, q1_plane,
+                          lambda cols: keys[:, 2 * cols.start : 2 * cols.stop].bitcast(FP4X4), keys_plane, on_vector)[0]
 
         def token_bids(t, a):
             ga = keep.tile([P, I], F32, name=f"ga{t}")
@@ -151,23 +153,30 @@ def tile_attend_pairwinners_twoq_mixed_kernel(
             nc.scalar.activation(gb[:], b[:].indirect(list_b[:]), COPY)
             return gb[:]
 
-        def bids(t, looked_up, ga):
+        def bids(engine, t, looked_up, ga):
             w = keep.tile([P, I], F32, name=f"w{t}")
-            nc.vector.tensor_tensor(w[:], looked_up, ga[:], ALU.add)
+            engine.tensor_tensor(w[:], looked_up, ga[:], ALU.add)
             return w
 
         def winners(t, w):
             m2 = keep.tile([P, J], F32, name=f"m2_{t}")
             pairs = w[:].rearrange("p (j two) -> p j two", two=2)
-            nc.vector.tensor_tensor(m2[:], pairs[:, :, 0], pairs[:, :, 1], ALU.max)
+            if t < PACK - 1:
+                nc.vector.tensor_tensor(m2[:], pairs[:, :, 0], pairs[:, :, 1], ALU.max)
+            else:
+                nc.vector.tensor_reduce(m2[:], pairs, mybir.AxisListType.X, ALU.max)
             return m2
 
         def place(t, m2):
             nc.vector.tensor_copy(placed[t % 2][:].indirect(list_f[:]), m2[:])
 
-        def raise_notes(t, b):
-            cc = keep.tile([P, U], F32, name=f"cc{t}", tag=f"a{(t + 1) % PACK}")
-            nc.vector.tensor_tensor(cc[:], b[:], placed[t % 2][:], ALU.add)
+        def raise_notes(t, b, banks):
+            cc = keep.tile([P, U], F32, name=f"cc{t}")
+            if t == 0:
+                nc.vector.tensor_tensor(cc[:], b[:], placed[t % 2][:], ALU.add)
+            else:
+                for cols, acc in banks:
+                    nc.vector.tensor_tensor(cc[:, cols], acc[:], placed[t % 2][:, cols], ALU.add)
             return cc
 
         n = I // HALVES
@@ -181,9 +190,9 @@ def tile_attend_pairwinners_twoq_mixed_kernel(
             nc.scalar.activation(gc[:], standing(cc, cols), COPY)
             return gc[:]
 
-        def results(name, looked_up, w, cols):
+        def results(engine, name, looked_up, w, cols):
             g = keep.tile([P, cols.stop - cols.start], F32, name=name)
-            nc.vector.tensor_tensor(g[:], looked_up, w[:, cols], ALU.subtract)
+            engine.tensor_tensor(g[:], looked_up, w[:, cols], ALU.subtract)
             return g
 
         def weigh(t, g, cols):
@@ -194,13 +203,14 @@ def tile_attend_pairwinners_twoq_mixed_kernel(
         ga = {0: token_bids(0, token_scores(0))}
         q2_codes, q2_plane = quantise_query("q2", q2_raw)
         ga[1] = token_bids(1, token_scores(1))
-        b = {0: note_scores(0, True)}
-        w = {0: bids(0, b[0][:].indirect(list_b[:]), ga[0])}
+        b, banks = {}, {}
+        b[0], banks[0] = note_scores(0, True)
+        w = {0: bids(nc.vector, 0, b[0][:].indirect(list_b[:]), ga[0])}
         gb = {}
         for t in range(1, PACK):
             if t > 1:
-                a = token_scores(t)
-            b[t] = note_scores(t)
+                a = token_scores(t, t == 2)
+            b[t], banks[t] = note_scores(t)
             gb[t] = note_bids(t, b[t])
             if t > 1:
                 ga[t] = token_bids(t, a)
@@ -209,19 +219,18 @@ def tile_attend_pairwinners_twoq_mixed_kernel(
         fetched = {}
         for t in range(last):
             place(t, m2)
-            w[t + 1] = bids(t + 1, gb[t + 1], ga[t + 1])
-            cc = raise_notes(t, b[t])
+            w[t + 1] = bids(nc.gpsimd, t + 1, gb[t + 1], ga[t + 1])
+            cc = raise_notes(t, b[t], banks[t])
             m2 = winners(t + 1, w[t + 1])
             fetched[t] = fetch(f"gc{t}", cc, every)
+        place(last, m2)
         for t in range(last):
-            if t == last - 1:
-                place(last, m2)
-            weigh(t, results(f"g{t}", fetched[t], w[t], every), every)
-        cc = raise_notes(last, b[last])
+            weigh(t, results(nc.gpsimd, f"g{t}", fetched[t], w[t], every), every)
+        cc = raise_notes(last, b[last], banks[last])
         first, second = slice(0, n), slice(n, I)
         fetched_second = fetch("gc_second", cc, second)
-        weigh(last, results("g_first", standing(cc, first), w[last], first), first)
-        weigh(last, results("g_second", fetched_second, w[last], second), second)
+        weigh(last, results(nc.vector, "g_first", standing(cc, first), w[last], first), first)
+        weigh(last, results(nc.vector, "g_second", fetched_second, w[last], second), second)
 
         for h in range(HALVES):
             cols = slice(h * n, (h + 1) * n)
@@ -237,7 +246,7 @@ def tile_attend_pairwinners_twoq_mixed_kernel(
             )
             for c in range(E // P):
                 chans = slice(c * P, (c + 1) * P)
-                acc = psum.tile([P, n], F32, name=f"acc_out{h}_{c}", tag=f"bank{2 * h + c}")
+                acc = psum.tile([P, n], F32, name=f"acc_out{h}_{c}", tag=f"bank{4 + 2 * h + c}")
                 nc.tensor.matmul_mx(
                     out=acc[:],
                     lhsT=mix[:, chans].bitcast(FP8X4),

from contextlib import ExitStack

import concourse.mybir as mybir

D, T, U, I, J, Q, E = 512, 1024, 1024, 512, 256, 512, 256
FLOPS = 2 * D * Q * T + 2 * D * Q * U + 2 * Q * E * I

F32 = mybir.dt.float32
BF16 = mybir.dt.bfloat16
I32 = mybir.dt.int32
U32 = mybir.dt.uint32
U16 = mybir.dt.uint16
U8 = mybir.dt.uint8
FP8X4 = mybir.dt.float8_e4m3fn_x4
FP4X4 = mybir.dt.float4_e2m1fn_x4
ALU = mybir.AluOpType
COPY = mybir.ActivationFunctionType.Copy

P = 128
PACK = 4
BANK = 512
HALVES = 2


def tile_attend_pairwinners_twoq_mixed_kernel(
    tc, query, query2, keys_words, keys_scales, notes_words, notes_scales, rowf,
    mix_words, mix_scales, offs, offs2, offs3, offs4, out,
):
    nc = tc.nc
    with ExitStack() as ctx:
        keep = ctx.enter_context(tc.tile_pool(name="keep", bufs=1))
        psum = ctx.enter_context(tc.psum_pool(name="psum", bufs=1))

        def zeroed_plane(engine, name, width):
            plane = keep.tile([P, width], U8, name=name, align_bytes=64)
            engine.memset(plane[:].bitcast(I32), 0)
            return plane

        def load_scales(queue, plane, scales):
            for quad in range(4):
                queue.dma_start(
                    out=plane[32 * quad : 32 * quad + 4, :].bitcast(I32),
                    in_=scales[0, 4 * quad : 4 * quad + 4, :].bitcast(I32),
                )

        def load_query(name, src):
            rows = src.rearrange("(p j) q -> p j q", j=PACK)
            halves = []
            for h in range(HALVES):
                raw = keep.tile([P, 2, Q], F32, name=f"{name}_raw{h}")
                nc.sync.dma_start(out=raw[:], in_=rows[:, 2 * h : 2 * h + 2, :])
                halves.append(raw)
            return halves

        def load_list(name, src, n):
            lst = keep.tile([P, n // 16], U16, name=name)
            nc.sync.dma_start(lst[:], src)
            return lst

        keys_plane = zeroed_plane(nc.vector, "keys_plane", T)
        notes_plane = zeroed_plane(nc.vector, "notes_plane", U)
        mix_plane = zeroed_plane(nc.vector, "mix_plane", E)
        placed = []
        for n in range(2):
            f1 = keep.tile([P, U], F32, name=f"placed{n}")
            nc.vector.memset(f1[:], 0.0)
            placed.append(f1)

        load_scales(nc.scalar, keys_plane, keys_scales)
        q1_raw = load_query("q1", query)
        keys = keep.tile([P, 2 * T], U8, name="keys", align_bytes=64)
        nc.sync.dma_start(out=keys[:].bitcast(I32), in_=keys_words[0].bitcast(I32))
        list_a = load_list("list_a", offs, I)
        q2_raw = load_query("q2", query2)
        load_scales(nc.sync, notes_plane, notes_scales)
        list_b = load_list("list_b", offs2, I)
        notes = keep.tile([P, U], U32, name="notes", align_bytes=64)
        nc.sync.dma_start(
            out=notes[:].bitcast(I32), in_=notes_words[0].rearrange("p n t -> p (n t)").bitcast(I32)
        )
        list_f = load_list("list_f", offs3, J)
        list_c = load_list("list_c", offs4, I)
        factor = keep.tile([P, PACK], F32, name="factor")
        nc.sync.dma_start(out=factor[:], in_=rowf.rearrange("(p t) o -> p (t o)", t=PACK))
        mix = keep.tile([P, E], U32, name="mix", align_bytes=64)
        nc.sync.dma_start(
            out=mix[:].bitcast(I32), in_=mix_words[0].rearrange("p n t -> p (n t)").bitcast(I32)
        )
        load_scales(nc.sync, mix_plane, mix_scales)

        def quantise_query(name, halves):
            grouped = keep.tile([P, PACK, P, PACK], BF16, name=f"{name}_grouped", align_bytes=64)
            for h, raw in enumerate(halves):
                nc.vector.tensor_copy(
                    out=grouped[:, :, :, 2 * h : 2 * h + 2].rearrange("p t m j -> p m j t"),
                    in_=raw[:].rearrange("p j (m t) -> p m j t", t=PACK),
                )
            codes = keep.tile([P, Q], U32, name=f"{name}_codes", align_bytes=64)
            plane = keep.tile([P, Q], U8, name=f"{name}_plane", align_bytes=64)
            flat = grouped[:].rearrange("p t m j -> p (t m j)")
            for t in range(PACK):
                cols = slice(t * P, (t + 1) * P)
                nc.vector.quantize_mx(
                    out=codes[:, cols].bitcast(FP8X4),
                    scales=plane[:, cols],
                    in_=flat[:, PACK * cols.start : PACK * cols.stop],
                )
            return codes, plane

        def scores(name, t, parts, codes, plane, moving, moving_plane, on_vector):
            whole = keep.tile([P, T], F32, name=f"{name}{t}", tag=f"{name}{t}")
            banks = []
            rows = slice(t * P, (t + 1) * P)
            for bank, cols in parts:
                acc = psum.tile([P, cols.stop - cols.start], F32, name=f"acc_{name}{t}_{bank}", tag=f"bank{bank}")
                nc.tensor.matmul_mx(
                    out=acc[:],
                    lhsT=codes[:, rows].bitcast(FP8X4),
                    lhsT_scale=plane[:, rows],
                    rhs=moving(cols),
                    rhs_scale=moving_plane[:, cols],
                    start=True,
                    stop=True,
                )
                if on_vector:
                    nc.vector.tensor_copy(whole[:, cols], acc[:])
                else:
                    nc.scalar.activation(whole[:, cols], acc[:], COPY)
                banks.append((cols, acc))
            return whole, banks

        def pair(k):
            return [(2 * k + c, slice(c * BANK, (c + 1) * BANK)) for c in range(2)]

        def token_scores(t, on_vector=False):
            return scores("a", t, pair(min(t, 2)), q1_codes, q1_plane,
                          lambda cols: keys[:, 2 * cols.start : 2 * cols.stop].bitcast(FP4X4), keys_plane, on_vector)[0]

        def token_bids(t, a):
            ga = keep.tile([P, I], F32, name=f"ga{t}")
            nc.scalar.activation(ga[:], a[:].indirect(list_a[:]), COPY)
            return ga

        def note_scores(t, on_vector=False):
            parts = pair((t + 2) % PACK)
            if t == 0:
                parts = [parts[0], (parts[1][0], slice(512, 768)), (0, slice(768, 1024))]
            return scores("b", t, parts, q2_codes, q2_plane,
                          lambda cols: notes[:, cols].bitcast(FP8X4), notes_plane, on_vector)

        def note_bids(t, b):
            gb = keep.tile([P, I], F32, name=f"gb{t}")
            nc.scalar.activation(gb[:], b[:].indirect(list_b[:]), COPY)
            return gb[:]

        def bids(engine, t, looked_up, ga):
            w = keep.tile([P, I], F32, name=f"w{t}")
            engine.tensor_tensor(w[:], looked_up, ga[:], ALU.add)
            return w

        def winners(t, w):
            m2 = keep.tile([P, J], F32, name=f"m2_{t}")
            pairs = w[:].rearrange("p (j two) -> p j two", two=2)
            if t < PACK - 1:
                nc.vector.tensor_tensor(m2[:], pairs[:, :, 0], pairs[:, :, 1], ALU.max)
            else:
                nc.vector.tensor_reduce(m2[:], pairs, mybir.AxisListType.X, ALU.max)
            return m2

        def place(t, m2):
            nc.vector.tensor_copy(placed[t % 2][:].indirect(list_f[:]), m2[:])

        def raise_notes(t, b, banks):
            cc = keep.tile([P, U], F32, name=f"cc{t}")
            if t == 0:
                nc.vector.tensor_tensor(cc[:], b[:], placed[t % 2][:], ALU.add)
            else:
                for cols, acc in banks:
                    nc.vector.tensor_tensor(cc[:, cols], acc[:], placed[t % 2][:, cols], ALU.add)
            return cc

        n = I // HALVES
        planes = keep.tile([P, PACK, I], BF16, name="planes")

        def standing(cc, cols):
            return cc[:].indirect(list_c[:, cols.start // 16 : cols.stop // 16])

        def fetch(name, cc, cols):
            gc = keep.tile([P, cols.stop - cols.start], F32, name=name)
            nc.scalar.activation(gc[:], standing(cc, cols), COPY)
            return gc[:]

        def results(engine, name, looked_up, w, cols):
            g = keep.tile([P, cols.stop - cols.start], F32, name=name)
            engine.tensor_tensor(g[:], looked_up, w[:, cols], ALU.subtract)
            return g

        def weigh(t, g, cols):
            nc.scalar.activation(planes[:, t, cols], g[:], COPY, scale=factor[:, t : t + 1])

        every = slice(0, I)
        q1_codes, q1_plane = quantise_query("q1", q1_raw)
        ga = {0: token_bids(0, token_scores(0))}
        q2_codes, q2_plane = quantise_query("q2", q2_raw)
        ga[1] = token_bids(1, token_scores(1))
        b, banks = {}, {}
        b[0], banks[0] = note_scores(0, True)
        w = {0: bids(nc.vector, 0, b[0][:].indirect(list_b[:]), ga[0])}
        gb = {}
        for t in range(1, PACK):
            if t > 1:
                a = token_scores(t, t == 2)
            b[t], banks[t] = note_scores(t)
            gb[t] = note_bids(t, b[t])
            if t > 1:
                ga[t] = token_bids(t, a)
        last = PACK - 1
        m2 = winners(0, w[0])
        fetched = {}
        for t in range(last):
            place(t, m2)
            w[t + 1] = bids(nc.gpsimd, t + 1, gb[t + 1], ga[t + 1])
            cc = raise_notes(t, b[t], banks[t])
            m2 = winners(t + 1, w[t + 1])
            fetched[t] = fetch(f"gc{t}", cc, every)
        place(last, m2)
        for t in range(last):
            weigh(t, results(nc.gpsimd, f"g{t}", fetched[t], w[t], every), every)
        cc = raise_notes(last, b[last], banks[last])
        first, second = slice(0, n), slice(n, I)
        fetched_second = fetch("gc_second", cc, second)
        weigh(last, results(nc.vector, "g_first", standing(cc, first), w[last], first), first)
        weigh(last, results(nc.vector, "g_second", fetched_second, w[last], second), second)

        for h in range(HALVES):
            cols = slice(h * n, (h + 1) * n)
            grouped = keep.tile([P, n, PACK], BF16, name=f"gw_grouped{h}", align_bytes=64)
            nc.vector.tensor_copy(
                out=grouped[:].rearrange("p (c i) t -> p c t i", i=4),
                in_=planes[:, :, cols].rearrange("p t (c i) -> p c t i", i=4),
            )
            codes = keep.tile([P, n], U32, name=f"gw_codes{h}", align_bytes=64)
            plane = keep.tile([P, n], U8, name=f"gw_plane{h}", align_bytes=64)
            nc.vector.quantize_mx(
                out=codes[:].bitcast(FP8X4), scales=plane[:], in_=grouped[:].rearrange("p i t -> p (i t)")
            )
            for c in range(E // P):
                chans = slice(c * P, (c + 1) * P)
                acc = psum.tile([P, n], F32, name=f"acc_out{h}_{c}", tag=f"bank{4 + 2 * h + c}")
                nc.tensor.matmul_mx(
                    out=acc[:],
                    lhsT=mix[:, chans].bitcast(FP8X4),
                    lhsT_scale=mix_plane[:, chans],
                    rhs=codes[:].bitcast(FP8X4),
                    rhs_scale=plane[:],
                    start=True,
                    stop=True,
                )
                result = keep.tile([P, n], F32, name=f"result{h}_{c}")
                if h == 1 and c == 1:
                    nc.vector.tensor_copy(result[:], acc[:])
                else:
                    nc.scalar.activation(result[:], acc[:], COPY)
                nc.sync.dma_start(out=out[chans, cols], in_=result[:])
